import numpy as np
import ml_dtypes


def mxq(x, axis, fmt="e4m3"):
    dtype, down = {"e4m3": (ml_dtypes.float8_e4m3fn, 7), "e5m2": (ml_dtypes.float8_e5m2, 14)}[fmt]
    v = np.moveaxis(np.asarray(x, np.float32).astype(ml_dtypes.bfloat16).astype(np.float64), axis, -1)
    blocks = v.reshape(v.shape[:-1] + (-1, 32))
    amax = np.abs(blocks).max(-1, keepdims=True)
    byte = np.maximum(np.where(amax > 0, np.frexp(amax)[1] - 1 + 127, 0) - down, 1)
    scale = np.exp2(byte - 127.0)
    codes = (blocks / scale).astype(np.float32).astype(dtype).astype(np.float64)
    return np.moveaxis((codes * scale).reshape(v.shape), -1, axis)


WIDE = False


def mx_kscale(k):
    if not WIDE:
        return np.ones(k)
    levels = np.array([10, -10, 5, -5, 0])
    if k % 512:
        return np.exp2(np.random.permutation(np.resize(levels, k // 32))).repeat(32)
    a = np.empty((k // 512, 16))
    for p in range(k // 512):
        a[p, :8] = np.random.permutation(np.resize(levels, 8))
        for g in range(8):
            far = levels[np.abs(levels - a[p, g]) >= 10]
            a[p, g + 8] = far[np.random.randint(len(far))]
    return np.exp2(a.ravel()).repeat(32)


def f64(x):
    return np.asarray(x).astype(np.float64)


def striped8(idx):
    return np.concatenate([v.reshape(-1, 16).T for v in idx]).astype(np.uint16)


def unstriped8(offs):
    return np.stack([offs[16 * g:16 * g + 16].T.reshape(-1) for g in range(8)]).astype(np.int64)


E2M1 = np.array([0.0, 0.5, 1.0, 1.5, 2.0, 3.0, 4.0, 6.0, -0.0, -0.5, -1.0, -1.5, -2.0, -3.0, -4.0, -6.0])


def pack_weight(w, fmt):
    k, n = w.shape
    w = f64(np.asarray(w, np.float32).astype(ml_dtypes.bfloat16)).reshape(k // 32, 32, n)
    amax = np.abs(w).max(1)
    if fmt == "e4m3":
        byte = np.frexp(amax)[1] - 1 + 127 - 7
    else:
        mant, ex = np.frexp(amax / 6.0)
        byte = np.where(mant > 0.5, ex, ex - 1) + 127
    byte = np.clip(np.where(amax > 0, byte, 1), 1, 254)
    scaled = (w * np.exp2(127.0 - byte)[:, None, :]).reshape(k, n).astype(np.float32)
    by_word = np.ascontiguousarray(scaled.reshape(k // 512, 128, 4, n).transpose(0, 1, 3, 2))
    if fmt == "e4m3":
        words = by_word.astype(ml_dtypes.float8_e4m3fn).view(np.uint8)
    else:
        c = by_word.astype(ml_dtypes.float4_e2m1fn).view(np.uint8) & 0xF
        words = (c[..., 0::2] | (c[..., 1::2] << 4)).reshape(k // 512, 128, 2 * n)
    return np.ascontiguousarray(words), np.ascontiguousarray(byte.astype(np.uint8).reshape(k // 512, 16, n))


def unpack_weight(words, scales, fmt):
    g, _, n = scales.shape
    words = np.ascontiguousarray(words).reshape(g, 128, n, -1)
    if fmt == "e4m3":
        vals = words.view(ml_dtypes.float8_e4m3fn).astype(np.float64)
    else:
        nib = np.empty((g, 128, n, 4), np.uint8)
        nib[..., 0::2] = words & 0xF
        nib[..., 1::2] = words >> 4
        vals = E2M1[nib]
    vals = vals * np.repeat(np.exp2(scales.astype(np.float64) - 127.0), 8, axis=1)[..., None]
    return vals.transpose(0, 1, 3, 2).reshape(g * 512, n)


def silu(v):
    return v / (1.0 + np.exp(-np.maximum(v, -700.0)))


K, M, T, S = 1536, 1024, 1024, 512


def setup_inputs():
    n = np.random.standard_normal
    s = mx_kscale(K)[:, None]
    w = n((K, M)) / np.sqrt(K) / s
    w4 = pack_weight(w, "e2m1")
    rest = w - unpack_weight(*w4, "e2m1")
    p_r8 = pack_weight(rest, "e4m3")
    return {
        "xT": (n((K, T)) * s).astype(np.float32),
        "w4_words": w4[0],
        "w4_scales": w4[1],
        "r8_words": p_r8[0],
        "r8_scales": p_r8[1],
        "wgt": np.repeat(np.random.uniform(0.5, 2.0, (8, S)), 16, axis=0).astype(np.float32),
        "b": (0.3 * n(1024)).astype(np.float32),
        "wgo": np.repeat(np.random.uniform(0.5, 2.0, (8, S)), 16, axis=0).astype(np.float32),
        "offs": striped8(np.stack([np.random.permutation(T)[:S] for _ in range(8)])),
        "offs2": striped8(np.stack([np.random.permutation(T)[:S] for _ in range(8)])),
    }


def reference(xT, w4_words, w4_scales, r8_words, r8_scales, wgt, b, wgo, offs, offs2):
    idx = unstriped8(offs)
    group = np.arange(K) % 512 // 64
    xg = f64(wgt)[np.arange(K) // 4 % 128] * f64(xT)[np.arange(K)[:, None], idx[group]]
    xT_ = mxq(xg, 0, "e4m3")
    w4_ = unpack_weight(w4_words, w4_scales, "e2m1")
    r8_ = unpack_weight(r8_words, r8_scales, "e4m3")
    y = w4_.T @ xT_ + r8_.T @ xT_
    place = unstriped8(offs2)[np.arange(M) % 128 // 16]
    out = np.zeros((M, T))
    out[np.arange(M)[:, None], place] = f64(wgo)[np.arange(M) % 128] * (silu(y + f64(b)[:, None]))
    return out

@@ -1,0 +1,201 @@
+from contextlib import ExitStack
+
+import concourse.mybir as mybir
+from concourse.masks import make_identity
+
+F32 = mybir.dt.float32
+BF16 = mybir.dt.bfloat16
+I32 = mybir.dt.int32
+U32 = mybir.dt.uint32
+U16 = mybir.dt.uint16
+U8 = mybir.dt.uint8
+FP8X4 = mybir.dt.float8_e4m3fn_x4
+FP4X4 = mybir.dt.float4_e2m1fn_x4
+MULT = mybir.AluOpType.mult
+SILU = mybir.ActivationFunctionType.Silu
+
+K, M, T, S = 1536, 1024, 1024, 512
+P = 128
+PACK = 4
+PASSES = K // (P * PACK)
+ROWS = M // P
+HALF = S // 2
+QUARTER = S // 4
+HALF_COLS = HALF // 16
+WINDOWS = 4
+FLOPS = 2 * 2 * K * M * S
+
+
+def tile_list_hboth_silu_kernel(
+    tc, xT, w4_words, w4_scales, r8_words, r8_scales, wgt, b, wgo, offs, offs2, out
+):
+    nc = tc.nc
+    with ExitStack() as ctx:
+        held = ctx.enter_context(tc.tile_pool(name="held", bufs=1))
+        psum = ctx.enter_context(tc.psum_pool(name="psum", bufs=1))
+
+        offs_t = held.tile([P, S // 16], U16, name="offs_t")
+        offs2_t = held.tile([P, S // 16], U16, name="offs2_t")
+        wgt_t = [held.tile([P, HALF], F32, name=f"wgt{h}") for h in range(2)]
+        wgo_t = held.tile([P, S], F32, name="wgo_t")
+        planes = [[held.tile([P, T], F32, name=f"x{a}_{i}") for i in range(PACK)] for a in range(PASSES)]
+        picked = [held.tile([P, PACK, S], F32, name=f"picked{a}") for a in range(PASSES)]
+        grouped = [held.tile([P, S, PACK], BF16, name=f"grouped{a}", align_bytes=64) for a in range(PASSES)]
+        codes = [held.tile([P, S], U32, name=f"codes{a}", align_bytes=64) for a in range(PASSES)]
+        scales = [held.tile([P, S], U8, name=f"scales{a}", align_bytes=64) for a in range(PASSES)]
+        w4_t = held.tile([P, PASSES, 2 * M], U8, name="w4_t", align_bytes=64)
+        r8_t = held.tile([P, PASSES, 4 * M], U8, name="r8_t", align_bytes=64)
+        w4_s = held.tile([P, PASSES, M], U8, name="w4_s", align_bytes=64)
+        r8_s = held.tile([P, PASSES, M], U8, name="r8_s", align_bytes=64)
+        windows = [held.tile([P, T], F32, name=f"window{w}") for w in range(WINDOWS)]
+        acts = [held.tile([P, S], F32, name=f"act{r}") for r in range(ROWS)]
+        b_rows = held.tile([P, P], F32, name="b_rows")
+        ident = held.tile([P, P], F32, name="ident")
+        bias = held.tile([P, ROWS], F32, name="bias")
+        dummy = held.tile([P, 2], F32, name="dummy")
+        banks = [psum.tile([P, 512], F32, name=f"bank{k}") for k in range(8)]
+
+        x_rows = xT.rearrange("(a p i) t -> a i p t", p=P, i=PACK)
+        w4_src = w4_words.bitcast(I32).rearrange("a p c -> p a c")
+        r8_src = r8_words.rearrange("a p n i -> a p (n i)").bitcast(I32).rearrange("a p c -> p a c")
+
+        nc.gpsimd.memset(dummy[:], 0.0)
+        nc.gpsimd.memset(w4_s[:].bitcast(I32), 0)
+        nc.gpsimd.memset(r8_s[:].bitcast(I32), 0)
+        nc.gpsimd.memset(b_rows[:], 0.0)
+        make_identity(nc, ident[:])
+        for w in range(WINDOWS):
+            nc.vector.memset(windows[w][:], 0.0)
+        nc.scalar.activation(dummy[:, 1:2], dummy[:, 0:1], SILU)
+
+        nc.sync.dma_start(offs_t[:], offs)
+        nc.sync.dma_start(wgt_t[0][:], wgt[:, 0:HALF])
+        nc.sync.dma_start(planes[0][0][:], x_rows[0, 0])
+        nc.sync.dma_start(wgt_t[1][:], wgt[:, HALF:S])
+        for i in range(1, PACK):
+            nc.sync.dma_start(planes[0][i][:], x_rows[0, i])
+        for i in range(PACK):
+            nc.sync.dma_start(planes[1][i][:], x_rows[1, i])
+        nc.sync.dma_start(b_rows[0:ROWS, :], b.rearrange("(r p) -> r p", p=P))
+        for q in range(4):
+            nc.sync.dma_start(
+                w4_s[32 * q : 32 * q + 4].bitcast(I32),
+                w4_scales[:, 4 * q : 4 * q + 4, :].bitcast(I32).rearrange("a r n -> r a n"),
+            )
+            nc.sync.dma_start(
+                r8_s[32 * q : 32 * q + 4].bitcast(I32),
+                r8_scales[:, 4 * q : 4 * q + 4, :].bitcast(I32).rearrange("a r n -> r a n"),
+            )
+
+        def load_weights(h):
+            c4 = slice(h * M // 4, (h + 1) * M // 4)
+            c8 = slice(h * M // 2, (h + 1) * M // 2)
+            nc.sync.dma_start(w4_t[:].bitcast(I32)[:, :, c4], w4_src[:, :, c4])
+            nc.sync.dma_start(r8_t[:].bitcast(I32)[:, :, c8], r8_src[:, :, c8])
+
+        load_weights(0)
+        for i in range(PACK):
+            nc.sync.dma_start(planes[2][i][:], x_rows[2, i])
+        nc.sync.dma_start(offs2_t[:], offs2)
+        nc.sync.dma_start(wgo_t[:], wgo)
+        load_weights(1)
+
+        nc.tensor.transpose(banks[7][:, 0:P], b_rows[:], ident[:])
+        nc.scalar.copy(bias[:], banks[7][:, 0:ROWS])
+
+        def gather(a, i, h):
+            nc.vector.tensor_tensor(
+                picked[a][:, i, h * HALF : (h + 1) * HALF],
+                planes[a][i][:].indirect(offs_t[:, h * HALF_COLS : (h + 1) * HALF_COLS]),
+                wgt_t[h][:],
+                MULT,
+            )
+
+        def interleave(a, c0, c1):
+            nc.scalar.copy(grouped[a][:, c0:c1, :], picked[a][:, :, c0:c1].rearrange("p i c -> p c i"))
+
+        def quantize(a, c0, c1):
+            nc.vector.quantize_mx(
+                out=codes[a][:, c0:c1].bitcast(FP8X4),
+                scales=scales[a][:, c0:c1],
+                in_=grouped[a][:, c0:c1, :].rearrange("p c i -> p (c i)"),
+            )
+
+        def multiply(dst, r, a, c0, c1):
+            for kind in range(2):
+                if kind == 0:
+                    lhsT = w4_t[:, a, 2 * P * r : 2 * P * (r + 1)].bitcast(FP4X4)
+                    lhsT_scale = w4_s[:, a, P * r : P * (r + 1)]
+                else:
+                    lhsT = r8_t[:, a, 4 * P * r : 4 * P * (r + 1)].bitcast(FP8X4)
+                    lhsT_scale = r8_s[:, a, P * r : P * (r + 1)]
+                nc.tensor.matmul_mx(
+                    out=dst,
+                    lhsT=lhsT,
+                    lhsT_scale=lhsT_scale,
+                    rhs=codes[a][:, c0:c1].bitcast(FP8X4),
+                    rhs_scale=scales[a][:, c0:c1],
+                    start=(a == 0 and kind == 0),
+                    stop=(a == PASSES - 1 and kind == 1),
+                )
+
+        early_a = [(banks[2 * r + k][:, 0:QUARTER], r, k * QUARTER, (k + 1) * QUARTER) for r in range(2) for k in range(2)]
+        early_full = [(banks[4][:], 2, 0, S), (banks[5][:], 3, 0, S)]
+
+        for a in range(PASSES - 1):
+            for i in range(PACK):
+                for h in range(2):
+                    gather(a, i, h)
+            interleave(a, 0, S)
+            quantize(a, 0, S)
+            for dst, r, c0, c1 in early_a + early_full:
+                multiply(dst, r, a, c0, c1)
+
+        a = PASSES - 1
+        for h in range(2):
+            for i in range(PACK):
+                gather(a, i, h)
+            if h == 0:
+                interleave(a, 0, HALF)
+                quantize(a, 0, HALF)
+                for dst, r, c0, c1 in early_a:
+                    multiply(dst, r, a, c0, c1)
+
+        def activate(r, c0, src):
+            c1 = c0 + src.shape[1]
+            nc.scalar.activation(acts[r][:, c0:c1], src, SILU, bias=bias[:, r : r + 1])
+
+        def scatter(r, h):
+            cols = slice(h * HALF, (h + 1) * HALF)
+            nc.vector.tensor_tensor(
+                windows[r % WINDOWS][:].indirect(offs2_t[:, h * HALF_COLS : (h + 1) * HALF_COLS]),
+                acts[r][:, cols],
+                wgo_t[:, cols],
+                MULT,
+            )
+            if h == 1:
+                nc.sync.dma_start(out[P * r : P * (r + 1), :], windows[r % WINDOWS][:])
+
+        for r in range(2):
+            for k in range(2):
+                activate(r, k * QUARTER, banks[2 * r + k][:, 0:QUARTER])
+        scatter(0, 0)
+        interleave(a, HALF, S)
+        quantize(a, HALF, S)
+        scatter(1, 0)
+        for r in range(2):
+            for k in range(2):
+                dst = banks[2 * r][:, (1 + k) * QUARTER : (2 + k) * QUARTER]
+                for c in range(PASSES):
+                    multiply(dst, r, c, HALF + k * QUARTER, HALF + (k + 1) * QUARTER)
+            activate(r, HALF, banks[2 * r][:, QUARTER : 3 * QUARTER])
+            scatter(r, 1)
+        late = {2: 4, 3: 5, 4: 6, 5: 7, 6: 1, 7: 3}
+        for r in range(2, ROWS):
+            bank = banks[late[r]]
+            for c in range(PASSES):
+                if r > 3 or c == PASSES - 1:
+                    multiply(bank[:], r, c, 0, S)
+            activate(r, 0, bank[:])
+            scatter(r, 0)
+            scatter(r, 1)

@@ -45,8 +45,7 @@ def tile_list_hboth_silu_kernel(
         scales = [held.tile([P, S], U8, name=f"scales{a}", align_bytes=64) for a in range(PASSES)]
         w4_t = held.tile([P, PASSES, 2 * M], U8, name="w4_t", align_bytes=64)
         r8_t = held.tile([P, PASSES, 4 * M], U8, name="r8_t", align_bytes=64)
-        w4_s = held.tile([P, PASSES, M], U8, name="w4_s", align_bytes=64)
-        r8_s = held.tile([P, PASSES, M], U8, name="r8_s", align_bytes=64)
+        w_s = held.tile([P, PASSES, M], U8, name="w_s", align_bytes=64)
         windows = [held.tile([P, T], F32, name=f"window{w}") for w in range(WINDOWS)]
         acts = [held.tile([P, S], F32, name=f"act{r}") for r in range(ROWS)]
         b_rows = held.tile([P, P], F32, name="b_rows")
@@ -60,8 +59,7 @@ def tile_list_hboth_silu_kernel(
         r8_src = r8_words.rearrange("a p n i -> a p (n i)").bitcast(I32).rearrange("a p c -> p a c")
 
         nc.gpsimd.memset(dummy[:], 0.0)
-        nc.gpsimd.memset(w4_s[:].bitcast(I32), 0)
-        nc.gpsimd.memset(r8_s[:].bitcast(I32), 0)
+        nc.gpsimd.memset(w_s[:].bitcast(I32), 0)
         nc.gpsimd.memset(b_rows[:], 0.0)
         make_identity(nc, ident[:])
         for w in range(WINDOWS):
@@ -74,31 +72,31 @@ def tile_list_hboth_silu_kernel(
         nc.sync.dma_start(wgt_t[1][:], wgt[:, HALF:S])
         for i in range(1, PACK):
             nc.sync.dma_start(planes[0][i][:], x_rows[0, i])
-        for i in range(PACK):
-            nc.sync.dma_start(planes[1][i][:], x_rows[1, i])
+        nc.sync.dma_start(offs2_t[:], offs2)
         nc.sync.dma_start(b_rows[0:ROWS, :], b.rearrange("(r p) -> r p", p=P))
+        for a in range(1, PASSES):
+            for i in range(PACK):
+                nc.sync.dma_start(planes[a][i][:], x_rows[a, i])
         for q in range(4):
             nc.sync.dma_start(
-                w4_s[32 * q : 32 * q + 4].bitcast(I32),
+                w_s[32 * q : 32 * q + 4].bitcast(I32),
                 w4_scales[:, 4 * q : 4 * q + 4, :].bitcast(I32).rearrange("a r n -> r a n"),
             )
             nc.sync.dma_start(
-                r8_s[32 * q : 32 * q + 4].bitcast(I32),
+                w_s[32 * q + 4 : 32 * q + 8].bitcast(I32),
                 r8_scales[:, 4 * q : 4 * q + 4, :].bitcast(I32).rearrange("a r n -> r a n"),
             )
 
         def load_weights(h):
-            c4 = slice(h * M // 4, (h + 1) * M // 4)
-            c8 = slice(h * M // 2, (h + 1) * M // 2)
+            c4 = slice(h * M // 8, (h + 1) * M // 8)
+            c8 = slice(h * M // 4, (h + 1) * M // 4)
             nc.sync.dma_start(w4_t[:].bitcast(I32)[:, :, c4], w4_src[:, :, c4])
             nc.sync.dma_start(r8_t[:].bitcast(I32)[:, :, c8], r8_src[:, :, c8])
 
         load_weights(0)
-        for i in range(PACK):
-            nc.sync.dma_start(planes[2][i][:], x_rows[2, i])
-        nc.sync.dma_start(offs2_t[:], offs2)
         nc.sync.dma_start(wgo_t[:], wgo)
-        load_weights(1)
+        for h in range(1, 4):
+            load_weights(h)
 
         nc.tensor.transpose(banks[7][:, 0:P], b_rows[:], ident[:])
         nc.scalar.copy(bias[:], banks[7][:, 0:ROWS])
@@ -125,10 +123,10 @@ def tile_list_hboth_silu_kernel(
             for kind in range(2):
                 if kind == 0:
                     lhsT = w4_t[:, a, 2 * P * r : 2 * P * (r + 1)].bitcast(FP4X4)
-                    lhsT_scale = w4_s[:, a, P * r : P * (r + 1)]
+                    lhsT_scale = w_s[:, a, P * r : P * (r + 1)]
                 else:
                     lhsT = r8_t[:, a, 4 * P * r : 4 * P * (r + 1)].bitcast(FP8X4)
-                    lhsT_scale = r8_s[:, a, P * r : P * (r + 1)]
+                    lhsT_scale = w_s[4:P, a, P * r : P * (r + 1)]
                 nc.tensor.matmul_mx(
                     out=dst,
                     lhsT=lhsT,
@@ -139,27 +137,34 @@ def tile_list_hboth_silu_kernel(
                     stop=(a == PASSES - 1 and kind == 1),
                 )
 
-        early_a = [(banks[2 * r + k][:, 0:QUARTER], r, k * QUARTER, (k + 1) * QUARTER) for r in range(2) for k in range(2)]
-        early_full = [(banks[4][:], 2, 0, S), (banks[5][:], 3, 0, S)]
+        early = [(banks[2 * r + k][:, 0:QUARTER], r, k * QUARTER, (k + 1) * QUARTER) for r in range(2) for k in range(2)]
+        last = PASSES - 1
 
-        for a in range(PASSES - 1):
-            for i in range(PACK):
-                for h in range(2):
-                    gather(a, i, h)
-            interleave(a, 0, S)
-            quantize(a, 0, S)
-            for dst, r, c0, c1 in early_a + early_full:
+        def multiply_early(a):
+            for dst, r, c0, c1 in early:
                 multiply(dst, r, a, c0, c1)
 
-        a = PASSES - 1
-        for h in range(2):
-            for i in range(PACK):
-                gather(a, i, h)
-            if h == 0:
-                interleave(a, 0, HALF)
-                quantize(a, 0, HALF)
-                for dst, r, c0, c1 in early_a:
-                    multiply(dst, r, a, c0, c1)
+        for i in range(PACK):
+            for h in range(2):
+                gather(0, i, h)
+        interleave(0, 0, S)
+        for i in range(PACK):
+            for h in range(2):
+                gather(1, i, h)
+        quantize(0, 0, S)
+        multiply_early(0)
+        interleave(1, 0, S)
+        for i in range(PACK):
+            gather(last, i, 0)
+        quantize(1, 0, S)
+        multiply_early(1)
+        interleave(last, 0, HALF)
+        gather(last, 0, 1)
+        gather(last, 1, 1)
+        gather(last, 2, 1)
+        quantize(last, 0, HALF)
+        multiply_early(last)
+        gather(last, 3, 1)
 
         def activate(r, c0, src):
             c1 = c0 + src.shape[1]
@@ -176,26 +181,28 @@ def tile_list_hboth_silu_kernel(
             if h == 1:
                 nc.sync.dma_start(out[P * r : P * (r + 1), :], windows[r % WINDOWS][:])
 
+        def late(r, dst, c0, c1):
+            for a in range(PASSES):
+                multiply(dst, r, a, c0, c1)
+
         for r in range(2):
             for k in range(2):
                 activate(r, k * QUARTER, banks[2 * r + k][:, 0:QUARTER])
         scatter(0, 0)
-        interleave(a, HALF, S)
-        quantize(a, HALF, S)
+        interleave(last, HALF, S)
+        quantize(last, HALF, S)
         scatter(1, 0)
         for r in range(2):
             for k in range(2):
-                dst = banks[2 * r][:, (1 + k) * QUARTER : (2 + k) * QUARTER]
-                for c in range(PASSES):
-                    multiply(dst, r, c, HALF + k * QUARTER, HALF + (k + 1) * QUARTER)
-            activate(r, HALF, banks[2 * r][:, QUARTER : 3 * QUARTER])
+                late(r, banks[4 + r][:, k * QUARTER : (k + 1) * QUARTER], HALF + k * QUARTER, HALF + (k + 1) * QUARTER)
+            activate(r, HALF, banks[4 + r][:, 0:HALF])
             scatter(r, 1)
-        late = {2: 4, 3: 5, 4: 6, 5: 7, 6: 1, 7: 3}
-        for r in range(2, ROWS):
-            bank = banks[late[r]]
-            for c in range(PASSES):
-                if r > 3 or c == PASSES - 1:
-                    multiply(bank[:], r, c, 0, S)
-            activate(r, 0, bank[:])
-            scatter(r, 0)
-            scatter(r, 1)
+        bank_of = (6, 7, 0, 1, 2, 3)
+        for r0 in range(2, ROWS, 2):
+            for r in (r0, r0 + 1):
+                bank = banks[bank_of[r - 2]]
+                late(r, bank[:], 0, S)
+                activate(r, 0, bank[:])
+            for h in range(2):
+                for r in (r0, r0 + 1):
+                    scatter(r, h)

@@ -60,7 +60,14 @@ def tile_list_hboth_silu_kernel(
 
         nc.gpsimd.memset(dummy[:], 0.0)
         nc.gpsimd.memset(w_s[:].bitcast(I32), 0)
+        for q in range(4):
+            for first, src in ((0, w4_scales), (4, r8_scales)):
+                nc.gpsimd.dma_start(
+                    w_s[32 * q + first : 32 * q + first + 4].bitcast(I32),
+                    src[:, 4 * q : 4 * q + 4, :].bitcast(I32).rearrange("a r n -> r a n"),
+                )
         nc.gpsimd.memset(b_rows[:], 0.0)
+        nc.gpsimd.dma_start(b_rows[0:ROWS, :], b.rearrange("(r p) -> r p", p=P))
         make_identity(nc, ident[:])
         for w in range(WINDOWS):
             nc.vector.memset(windows[w][:], 0.0)
@@ -73,19 +80,9 @@ def tile_list_hboth_silu_kernel(
         for i in range(1, PACK):
             nc.sync.dma_start(planes[0][i][:], x_rows[0, i])
         nc.sync.dma_start(offs2_t[:], offs2)
-        nc.sync.dma_start(b_rows[0:ROWS, :], b.rearrange("(r p) -> r p", p=P))
         for a in range(1, PASSES):
             for i in range(PACK):
                 nc.sync.dma_start(planes[a][i][:], x_rows[a, i])
-        for q in range(4):
-            nc.sync.dma_start(
-                w_s[32 * q : 32 * q + 4].bitcast(I32),
-                w4_scales[:, 4 * q : 4 * q + 4, :].bitcast(I32).rearrange("a r n -> r a n"),
-            )
-            nc.sync.dma_start(
-                w_s[32 * q + 4 : 32 * q + 8].bitcast(I32),
-                r8_scales[:, 4 * q : 4 * q + 4, :].bitcast(I32).rearrange("a r n -> r a n"),
-            )
 
         def load_weights(h):
             c4 = slice(h * M // 8, (h + 1) * M // 8)
@@ -137,34 +134,39 @@ def tile_list_hboth_silu_kernel(
                     stop=(a == PASSES - 1 and kind == 1),
                 )
 
-        early = [(banks[2 * r + k][:, 0:QUARTER], r, k * QUARTER, (k + 1) * QUARTER) for r in range(2) for k in range(2)]
         last = PASSES - 1
+        open_a = [(0, 0, 0), (1, 0, 1), (2, 1, 0), (3, 1, 1)]
+        open_b = [(4, 0, 2), (5, 0, 3)]
 
-        def multiply_early(a):
-            for dst, r, c0, c1 in early:
-                multiply(dst, r, a, c0, c1)
+        def multiply_open(groups, a):
+            for k, r, q in groups:
+                multiply(banks[k][:, 0:QUARTER], r, a, q * QUARTER, (q + 1) * QUARTER)
 
+        LAG = 4
+        for n in range(PASSES * PACK):
+            a, i = n // PACK, n % PACK
+            gather(a, i, 0)
+            if n == PACK + 2 or n == 2 * PACK + 2:
+                quantize(a - 1, 0, HALF)
+                multiply_open(open_a, a - 1)
+            if i == PACK - 1:
+                for c0 in (0, QUARTER) if a == last else (0,):
+                    interleave(a, c0, c0 + (QUARTER if a == last else HALF))
+            if n >= LAG:
+                a, i = (n - LAG) // PACK, (n - LAG) % PACK
+                gather(a, i, 1)
+                if i == PACK - 1:
+                    interleave(a, HALF, S)
+        quantize(0, HALF, S)
+        multiply_open(open_b, 0)
         for i in range(PACK):
-            for h in range(2):
-                gather(0, i, h)
-        interleave(0, 0, S)
-        for i in range(PACK):
-            for h in range(2):
-                gather(1, i, h)
-        quantize(0, 0, S)
-        multiply_early(0)
-        interleave(1, 0, S)
-        for i in range(PACK):
-            gather(last, i, 0)
-        quantize(1, 0, S)
-        multiply_early(1)
-        interleave(last, 0, HALF)
-        gather(last, 0, 1)
-        gather(last, 1, 1)
-        gather(last, 2, 1)
-        quantize(last, 0, HALF)
-        multiply_early(last)
-        gather(last, 3, 1)
+            gather(last, i, 1)
+            if i < 2:
+                quantize(last, i * QUARTER, (i + 1) * QUARTER)
+                multiply_open([g for g in open_a if g[2] == i], last)
+        interleave(last, HALF, S)
+        quantize(1, HALF, S)
+        multiply_open(open_b, 1)
 
         def activate(r, c0, src):
             c1 = c0 + src.shape[1]
@@ -189,15 +191,17 @@ def tile_list_hboth_silu_kernel(
             for k in range(2):
                 activate(r, k * QUARTER, banks[2 * r + k][:, 0:QUARTER])
         scatter(0, 0)
-        interleave(last, HALF, S)
         quantize(last, HALF, S)
+        multiply_open(open_b, last)
+        for k in range(2):
+            activate(0, HALF + k * QUARTER, banks[4 + k][:, 0:QUARTER])
         scatter(1, 0)
-        for r in range(2):
-            for k in range(2):
-                late(r, banks[4 + r][:, k * QUARTER : (k + 1) * QUARTER], HALF + k * QUARTER, HALF + (k + 1) * QUARTER)
-            activate(r, HALF, banks[4 + r][:, 0:HALF])
-            scatter(r, 1)
-        bank_of = (6, 7, 0, 1, 2, 3)
+        scatter(0, 1)
+        for k in range(2):
+            late(1, banks[6][:, k * QUARTER : (k + 1) * QUARTER], HALF + k * QUARTER, HALF + (k + 1) * QUARTER)
+        activate(1, HALF, banks[6][:, 0:HALF])
+        scatter(1, 1)
+        bank_of = (7, 0, 1, 2, 3, 4)
         for r0 in range(2, ROWS, 2):
             for r in (r0, r0 + 1):
                 bank = banks[bank_of[r - 2]]

@@ -37,7 +37,7 @@ def tile_list_hboth_silu_kernel(
         offs_t = held.tile([P, S // 16], U16, name="offs_t")
         offs2_t = held.tile([P, S // 16], U16, name="offs2_t")
         wgt_t = [held.tile([P, HALF], F32, name=f"wgt{h}") for h in range(2)]
-        wgo_t = held.tile([P, S], F32, name="wgo_t")
+        wgo_t = [held.tile([P, HALF], F32, name=f"wgo{h}") for h in range(2)]
         planes = [[held.tile([P, T], F32, name=f"x{a}_{i}") for i in range(PACK)] for a in range(PASSES)]
         picked = [held.tile([P, PACK, S], F32, name=f"picked{a}") for a in range(PASSES)]
         grouped = [held.tile([P, S, PACK], BF16, name=f"grouped{a}", align_bytes=64) for a in range(PASSES)]
@@ -91,9 +91,10 @@ def tile_list_hboth_silu_kernel(
             nc.sync.dma_start(r8_t[:].bitcast(I32)[:, :, c8], r8_src[:, :, c8])
 
         load_weights(0)
-        nc.sync.dma_start(wgo_t[:], wgo)
-        for h in range(1, 4):
-            load_weights(h)
+        for h in range(2):
+            nc.sync.dma_start(wgo_t[h][:], wgo[:, h * HALF : (h + 1) * HALF])
+            load_weights(1 + h)
+        load_weights(3)
 
         nc.tensor.transpose(banks[7][:, 0:P], b_rows[:], ident[:])
         nc.scalar.copy(bias[:], banks[7][:, 0:ROWS])
@@ -135,7 +136,7 @@ def tile_list_hboth_silu_kernel(
                 )
 
         last = PASSES - 1
-        open_a = [(0, 0, 0), (1, 0, 1), (2, 1, 0), (3, 1, 1)]
+        open_a = [(0, 0, 0), (1, 0, 1)]
         open_b = [(4, 0, 2), (5, 0, 3)]
 
         def multiply_open(groups, a):
@@ -150,8 +151,7 @@ def tile_list_hboth_silu_kernel(
                 quantize(a - 1, 0, HALF)
                 multiply_open(open_a, a - 1)
             if i == PACK - 1:
-                for c0 in (0, QUARTER) if a == last else (0,):
-                    interleave(a, c0, c0 + (QUARTER if a == last else HALF))
+                interleave(a, 0, QUARTER if a == last else HALF)
             if n >= LAG:
                 a, i = (n - LAG) // PACK, (n - LAG) % PACK
                 gather(a, i, 1)
@@ -159,11 +159,14 @@ def tile_list_hboth_silu_kernel(
                     interleave(a, HALF, S)
         quantize(0, HALF, S)
         multiply_open(open_b, 0)
+        nc.vector.tensor_copy(
+            grouped[last][:, QUARTER:HALF, :], picked[last][:, :, QUARTER:HALF].rearrange("p i c -> p c i")
+        )
         for i in range(PACK):
             gather(last, i, 1)
-            if i < 2:
-                quantize(last, i * QUARTER, (i + 1) * QUARTER)
-                multiply_open([g for g in open_a if g[2] == i], last)
+            if i == 0:
+                quantize(last, 0, HALF)
+                multiply_open(open_a, last)
         interleave(last, HALF, S)
         quantize(1, HALF, S)
         multiply_open(open_b, 1)
@@ -177,7 +180,7 @@ def tile_list_hboth_silu_kernel(
             nc.vector.tensor_tensor(
                 windows[r % WINDOWS][:].indirect(offs2_t[:, h * HALF_COLS : (h + 1) * HALF_COLS]),
                 acts[r][:, cols],
-                wgo_t[:, cols],
+                wgo_t[h][:],
                 MULT,
             )
             if h == 1:
@@ -187,10 +190,12 @@ def tile_list_hboth_silu_kernel(
             for a in range(PASSES):
                 multiply(dst, r, a, c0, c1)
 
-        for r in range(2):
-            for k in range(2):
-                activate(r, k * QUARTER, banks[2 * r + k][:, 0:QUARTER])
+        for k in range(2):
+            activate(0, k * QUARTER, banks[k][:, 0:QUARTER])
         scatter(0, 0)
+        for k in range(2):
+            late(1, banks[2][:, k * QUARTER : (k + 1) * QUARTER], k * QUARTER, (k + 1) * QUARTER)
+        activate(1, 0, banks[2][:, 0:HALF])
         quantize(last, HALF, S)
         multiply_open(open_b, last)
         for k in range(2):

@@ -60,18 +60,18 @@ def tile_list_hboth_silu_kernel(
 
         nc.gpsimd.memset(dummy[:], 0.0)
         nc.gpsimd.memset(w_s[:].bitcast(I32), 0)
-        for q in range(4):
-            for first, src in ((0, w4_scales), (4, r8_scales)):
-                nc.gpsimd.dma_start(
-                    w_s[32 * q + first : 32 * q + first + 4].bitcast(I32),
-                    src[:, 4 * q : 4 * q + 4, :].bitcast(I32).rearrange("a r n -> r a n"),
-                )
         nc.gpsimd.memset(b_rows[:], 0.0)
-        nc.gpsimd.dma_start(b_rows[0:ROWS, :], b.rearrange("(r p) -> r p", p=P))
         make_identity(nc, ident[:])
         for w in range(WINDOWS):
             nc.vector.memset(windows[w][:], 0.0)
         nc.scalar.activation(dummy[:, 1:2], dummy[:, 0:1], SILU)
+
+        for q in range(4):
+            for first, src in ((0, w4_scales), (4, r8_scales)):
+                nc.scalar.dma_start(
+                    w_s[32 * q + first : 32 * q + first + 4].bitcast(I32),
+                    src[:, 4 * q : 4 * q + 4, :].bitcast(I32).rearrange("a r n -> r a n"),
+                )
 
         nc.sync.dma_start(offs_t[:], offs)
         nc.sync.dma_start(wgt_t[0][:], wgt[:, 0:HALF])
@@ -80,6 +80,7 @@ def tile_list_hboth_silu_kernel(
         for i in range(1, PACK):
             nc.sync.dma_start(planes[0][i][:], x_rows[0, i])
         nc.sync.dma_start(offs2_t[:], offs2)
+        nc.sync.dma_start(b_rows[0:ROWS, :], b.rearrange("(r p) -> r p", p=P))
         for a in range(1, PASSES):
             for i in range(PACK):
                 nc.sync.dma_start(planes[a][i][:], x_rows[a, i])
@@ -107,8 +108,14 @@ def tile_list_hboth_silu_kernel(
                 MULT,
             )
 
+        def interleaved(a, c0, c1):
+            return (
+                grouped[a][:, c0:c1, :].rearrange("p (c j) i -> p c i j", j=4),
+                picked[a][:, :, c0:c1].rearrange("p i (c j) -> p c i j", j=4),
+            )
+
         def interleave(a, c0, c1):
-            nc.scalar.copy(grouped[a][:, c0:c1, :], picked[a][:, :, c0:c1].rearrange("p i c -> p c i"))
+            nc.scalar.copy(*interleaved(a, c0, c1))
 
         def quantize(a, c0, c1):
             nc.vector.quantize_mx(
@@ -147,9 +154,12 @@ def tile_list_hboth_silu_kernel(
         for n in range(PASSES * PACK):
             a, i = n // PACK, n % PACK
             gather(a, i, 0)
-            if n == PACK + 2 or n == 2 * PACK + 2:
-                quantize(a - 1, 0, HALF)
-                multiply_open(open_a, a - 1)
+            if n == 2 * PACK:
+                quantize(0, 0, S)
+                multiply_open(open_a, 0)
+            if n == 2 * PACK + 2:
+                quantize(1, 0, HALF)
+                multiply_open(open_a, 1)
             if i == PACK - 1:
                 interleave(a, 0, QUARTER if a == last else HALF)
             if n >= LAG:
@@ -157,11 +167,7 @@ def tile_list_hboth_silu_kernel(
                 gather(a, i, 1)
                 if i == PACK - 1:
                     interleave(a, HALF, S)
-        quantize(0, HALF, S)
-        multiply_open(open_b, 0)
-        nc.vector.tensor_copy(
-            grouped[last][:, QUARTER:HALF, :], picked[last][:, :, QUARTER:HALF].rearrange("p i c -> p c i")
-        )
+        nc.vector.tensor_copy(*interleaved(last, QUARTER, HALF))
         for i in range(PACK):
             gather(last, i, 1)
             if i == 0:
@@ -169,7 +175,8 @@ def tile_list_hboth_silu_kernel(
                 multiply_open(open_a, last)
         interleave(last, HALF, S)
         quantize(1, HALF, S)
-        multiply_open(open_b, 1)
+        for a in range(last):
+            multiply_open(open_b, a)
 
         def activate(r, c0, src):
             c1 = c0 + src.shape[1]

from contextlib import ExitStack

import concourse.mybir as mybir
from concourse.masks import make_identity

F32 = mybir.dt.float32
BF16 = mybir.dt.bfloat16
I32 = mybir.dt.int32
U32 = mybir.dt.uint32
U16 = mybir.dt.uint16
U8 = mybir.dt.uint8
FP8X4 = mybir.dt.float8_e4m3fn_x4
FP4X4 = mybir.dt.float4_e2m1fn_x4
MULT = mybir.AluOpType.mult
SILU = mybir.ActivationFunctionType.Silu

K, M, T, S = 1536, 1024, 1024, 512
P = 128
PACK = 4
PASSES = K // (P * PACK)
ROWS = M // P
HALF = S // 2
QUARTER = S // 4
HALF_COLS = HALF // 16
WINDOWS = 4
FLOPS = 2 * 2 * K * M * S


def tile_list_hboth_silu_kernel(
    tc, xT, w4_words, w4_scales, r8_words, r8_scales, wgt, b, wgo, offs, offs2, out
):
    nc = tc.nc
    with ExitStack() as ctx:
        held = ctx.enter_context(tc.tile_pool(name="held", bufs=1))
        psum = ctx.enter_context(tc.psum_pool(name="psum", bufs=1))

        offs_t = held.tile([P, S // 16], U16, name="offs_t")
        offs2_t = held.tile([P, S // 16], U16, name="offs2_t")
        wgt_t = [held.tile([P, HALF], F32, name=f"wgt{h}") for h in range(2)]
        wgo_t = [held.tile([P, HALF], F32, name=f"wgo{h}") for h in range(2)]
        planes = [[held.tile([P, T], F32, name=f"x{a}_{i}") for i in range(PACK)] for a in range(PASSES)]
        picked = [held.tile([P, PACK, S], F32, name=f"picked{a}") for a in range(PASSES)]
        grouped = [held.tile([P, S, PACK], BF16, name=f"grouped{a}", align_bytes=64) for a in range(PASSES)]
        codes = [held.tile([P, S], U32, name=f"codes{a}", align_bytes=64) for a in range(PASSES)]
        scales = [held.tile([P, S], U8, name=f"scales{a}", align_bytes=64) for a in range(PASSES)]
        w4_t = held.tile([P, PASSES, 2 * M], U8, name="w4_t", align_bytes=64)
        r8_t = held.tile([P, PASSES, 4 * M], U8, name="r8_t", align_bytes=64)
        w_s = held.tile([P, PASSES, M], U8, name="w_s", align_bytes=64)
        windows = [held.tile([P, T], F32, name=f"window{w}") for w in range(WINDOWS)]
        acts = [held.tile([P, S], F32, name=f"act{r}") for r in range(ROWS)]
        b_rows = held.tile([P, P], F32, name="b_rows")
        ident = held.tile([P, P], F32, name="ident")
        bias = held.tile([P, ROWS], F32, name="bias")
        dummy = held.tile([P, 2], F32, name="dummy")
        banks = [psum.tile([P, 512], F32, name=f"bank{k}") for k in range(8)]

        x_rows = xT.rearrange("(a p i) t -> a i p t", p=P, i=PACK)
        w4_src = w4_words.bitcast(I32).rearrange("a p c -> p a c")
        r8_src = r8_words.rearrange("a p n i -> a p (n i)").bitcast(I32).rearrange("a p c -> p a c")

        nc.gpsimd.memset(dummy[:], 0.0)
        nc.gpsimd.memset(w_s[:].bitcast(I32), 0)
        nc.gpsimd.memset(b_rows[:], 0.0)
        make_identity(nc, ident[:])
        for w in range(WINDOWS):
            nc.vector.memset(windows[w][:], 0.0)
        nc.scalar.activation(dummy[:, 1:2], dummy[:, 0:1], SILU)

        for q in range(4):
            for first, src in ((0, w4_scales), (4, r8_scales)):
                nc.scalar.dma_start(
                    w_s[32 * q + first : 32 * q + first + 4].bitcast(I32),
                    src[:, 4 * q : 4 * q + 4, :].bitcast(I32).rearrange("a r n -> r a n"),
                )

        nc.sync.dma_start(offs_t[:], offs)
        nc.sync.dma_start(wgt_t[0][:], wgt[:, 0:HALF])
        nc.sync.dma_start(planes[0][0][:], x_rows[0, 0])
        nc.sync.dma_start(wgt_t[1][:], wgt[:, HALF:S])
        for i in range(1, PACK):
            nc.sync.dma_start(planes[0][i][:], x_rows[0, i])
        nc.sync.dma_start(offs2_t[:], offs2)
        nc.sync.dma_start(b_rows[0:ROWS, :], b.rearrange("(r p) -> r p", p=P))
        for a in range(1, PASSES):
            for i in range(PACK):
                nc.sync.dma_start(planes[a][i][:], x_rows[a, i])

        def load_weights(h):
            c4 = slice(h * M // 8, (h + 1) * M // 8)
            c8 = slice(h * M // 4, (h + 1) * M // 4)
            nc.sync.dma_start(w4_t[:].bitcast(I32)[:, :, c4], w4_src[:, :, c4])
            nc.sync.dma_start(r8_t[:].bitcast(I32)[:, :, c8], r8_src[:, :, c8])

        load_weights(0)
        for h in range(2):
            nc.sync.dma_start(wgo_t[h][:], wgo[:, h * HALF : (h + 1) * HALF])
            load_weights(1 + h)
        load_weights(3)

        nc.tensor.transpose(banks[7][:, 0:P], b_rows[:], ident[:])
        nc.scalar.copy(bias[:], banks[7][:, 0:ROWS])

        def gather(a, i, h):
            nc.vector.tensor_tensor(
                picked[a][:, i, h * HALF : (h + 1) * HALF],
                planes[a][i][:].indirect(offs_t[:, h * HALF_COLS : (h + 1) * HALF_COLS]),
                wgt_t[h][:],
                MULT,
            )

        def interleaved(a, c0, c1):
            return (
                grouped[a][:, c0:c1, :].rearrange("p (c j) i -> p c i j", j=4),
                picked[a][:, :, c0:c1].rearrange("p i (c j) -> p c i j", j=4),
            )

        def interleave(a, c0, c1):
            nc.scalar.copy(*interleaved(a, c0, c1))

        def quantize(a, c0, c1):
            nc.vector.quantize_mx(
                out=codes[a][:, c0:c1].bitcast(FP8X4),
                scales=scales[a][:, c0:c1],
                in_=grouped[a][:, c0:c1, :].rearrange("p c i -> p (c i)"),
            )

        def multiply(dst, r, a, c0, c1):
            for kind in range(2):
                if kind == 0:
                    lhsT = w4_t[:, a, 2 * P * r : 2 * P * (r + 1)].bitcast(FP4X4)
                    lhsT_scale = w_s[:, a, P * r : P * (r + 1)]
                else:
                    lhsT = r8_t[:, a, 4 * P * r : 4 * P * (r + 1)].bitcast(FP8X4)
                    lhsT_scale = w_s[4:P, a, P * r : P * (r + 1)]
                nc.tensor.matmul_mx(
                    out=dst,
                    lhsT=lhsT,
                    lhsT_scale=lhsT_scale,
                    rhs=codes[a][:, c0:c1].bitcast(FP8X4),
                    rhs_scale=scales[a][:, c0:c1],
                    start=(a == 0 and kind == 0),
                    stop=(a == PASSES - 1 and kind == 1),
                )

        last = PASSES - 1
        open_a = [(0, 0, 0), (1, 0, 1)]
        open_b = [(4, 0, 2), (5, 0, 3)]

        def multiply_open(groups, a):
            for k, r, q in groups:
                multiply(banks[k][:, 0:QUARTER], r, a, q * QUARTER, (q + 1) * QUARTER)

        LAG = 4
        for n in range(PASSES * PACK):
            a, i = n // PACK, n % PACK
            gather(a, i, 0)
            if n == 2 * PACK:
                quantize(0, 0, S)
                multiply_open(open_a, 0)
            if n == 2 * PACK + 2:
                quantize(1, 0, HALF)
                multiply_open(open_a, 1)
            if i == PACK - 1:
                interleave(a, 0, QUARTER if a == last else HALF)
            if n >= LAG:
                a, i = (n - LAG) // PACK, (n - LAG) % PACK
                gather(a, i, 1)
                if i == PACK - 1:
                    interleave(a, HALF, S)
        nc.vector.tensor_copy(*interleaved(last, QUARTER, HALF))
        for i in range(PACK):
            gather(last, i, 1)
            if i == 0:
                quantize(last, 0, HALF)
                multiply_open(open_a, last)
        interleave(last, HALF, S)
        quantize(1, HALF, S)
        for a in range(last):
            multiply_open(open_b, a)

        def activate(r, c0, src):
            c1 = c0 + src.shape[1]
            nc.scalar.activation(acts[r][:, c0:c1], src, SILU, bias=bias[:, r : r + 1])

        def scatter(r, h):
            cols = slice(h * HALF, (h + 1) * HALF)
            nc.vector.tensor_tensor(
                windows[r % WINDOWS][:].indirect(offs2_t[:, h * HALF_COLS : (h + 1) * HALF_COLS]),
                acts[r][:, cols],
                wgo_t[h][:],
                MULT,
            )
            if h == 1:
                nc.sync.dma_start(out[P * r : P * (r + 1), :], windows[r % WINDOWS][:])

        def late(r, dst, c0, c1):
            for a in range(PASSES):
                multiply(dst, r, a, c0, c1)

        for k in range(2):
            activate(0, k * QUARTER, banks[k][:, 0:QUARTER])
        scatter(0, 0)
        for k in range(2):
            late(1, banks[2][:, k * QUARTER : (k + 1) * QUARTER], k * QUARTER, (k + 1) * QUARTER)
        activate(1, 0, banks[2][:, 0:HALF])
        quantize(last, HALF, S)
        multiply_open(open_b, last)
        for k in range(2):
            activate(0, HALF + k * QUARTER, banks[4 + k][:, 0:QUARTER])
        scatter(1, 0)
        scatter(0, 1)
        for k in range(2):
            late(1, banks[6][:, k * QUARTER : (k + 1) * QUARTER], HALF + k * QUARTER, HALF + (k + 1) * QUARTER)
        activate(1, HALF, banks[6][:, 0:HALF])
        scatter(1, 1)
        bank_of = (7, 0, 1, 2, 3, 4)
        for r0 in range(2, ROWS, 2):
            for r in (r0, r0 + 1):
                bank = banks[bank_of[r - 2]]
                late(r, bank[:], 0, S)
                activate(r, 0, bank[:])
            for h in range(2):
                for r in (r0, r0 + 1):
                    scatter(r, h)
